import numpy as np, ml_dtypes
CORES = [10,34,74,98]
N = 4
import mx_ref
BF = ml_dtypes.bfloat16
def entries(a):
    return np.ascontiguousarray(a.T).reshape(-1)
def table(e):
    return np.ascontiguousarray(np.reshape(e, (-1, 16)).T).astype(np.int32)
def cols(t, e):
    v = np.concatenate([t.reshape(128, -1, 4), np.zeros((128, 1, 4), BF)], axis=1)
    return np.ascontiguousarray(v[:, e]).reshape(128, -1)
def tile(rs):
    return np.stack(rs, axis=2).reshape(128, -1).astype(BF)
def cut(t, i, w=512):
    return t[:, w * i:w * i + w]
def rowtile(v, k):
    z = np.concatenate([v, np.zeros((1, v.shape[1]), BF)])
    return np.concatenate([np.ascontiguousarray(z[k[:, 4 * m:4 * m + 4]].transpose(0, 2, 1)).reshape(128, -1) for m in range(k.shape[1] // 4)], axis=1)
def f(rng, *shape):
    return mx_ref.flush((rng.standard_normal(shape, dtype=np.float32) * np.exp2(rng.integers(-2, 3, shape[:-1] + (1,)))).astype(BF))
def wide(rng, *shape, cols=0):
    v = rng.standard_normal(shape, dtype=np.float32) * np.exp2(rng.integers(-12, 13, shape)).astype(np.float32)
    if cols: v *= np.repeat(np.exp2(rng.integers(-cols, cols + 1, shape[:-2] + (1, shape[-1] // 4))) * (rng.random(shape[:-2] + (1, shape[-1] // 4)) > 0.0625), 4, axis=-1).astype(np.float32)
    return mx_ref.flush(v.astype(BF))
T, HU, ACT = 128, 1536, 512
def lists(rng, how=None):
    a = []
    for r in range(N):
        e = rng.permutation(HU)[:ACT]
        if how == "reversed": e = np.sort(e)[::-1]
        if how == "clustered": e = rng.integers(0, HU - ACT + 1) + np.arange(ACT)
        a.append(e)
    return {"act": np.stack([e.reshape(128, 4).astype(np.int32) for e in a]), "actc": np.stack([table(e) for e in a])}
def setup_inputs(rng):
    return {"x": f(rng, N, 128, 4 * T), "w1": f(rng, N, 128, 4 * HU), "w2": f(rng, N, HU, 512), **lists(rng)}
def setup_inputs_clustered(rng):
    return {**setup_inputs(rng), **lists(rng, "clustered")}
def setup_inputs_dead(rng):
    d = setup_inputs(rng); d["x"] = np.abs(d["x"])
    for r in range(N):
        k = d["act"][r].reshape(-1)[rng.permutation(ACT)[:ACT // 2]]
        w = d["w1"][r].reshape(128, HU, 4)
        w[:, k] = -np.abs(w[:, k])
        d["w1"][r] = w.reshape(128, -1)
    return d
def setup_inputs_giant(rng):
    d = setup_inputs(rng)
    for r in range(N):
        k = d["act"][r].reshape(-1)[rng.permutation(ACT)[:ACT // 32]]
        d["w2"][r, k] = (d["w2"][r, k].astype(np.float32) * np.float32(4096)).astype(BF)
    return d
def setup_inputs_reversed(rng):
    return {**setup_inputs(rng), **lists(rng, "reversed")}
def setup_inputs_spread(rng):
    d = setup_inputs(rng); d["x"] = wide(rng, N, 128, 4 * T); d["w2"] = wide(rng, N, HU, 512); return d
def check_inputs(d):
    b = []
    for r in range(N):
        e = d["act"][r].reshape(-1)
        if e.min() < 0 or e.max() >= HU or len(set(e.tolist())) != ACT: b.append("act")
        if (entries(d["actc"][r]) != e).any(): b.append("actc")
    return b
def reference(x, w1, w2, act, actc):
    y = np.zeros((N, 128, 4 * T), np.float32)
    X = [mx_ref.quantize(x[r]) for r in range(N)]
    for s in range(N):
        A = [mx_ref.quantize(cols(w1[s], act[s][:, b])) for b in range(4)]
        rows = rowtile(w2[s], act[s])
        B = [mx_ref.quantize(np.ascontiguousarray(cut(rows, o))) for o in range(4)]
        for r in range(N):
            H = mx_ref.quantize(tile([np.maximum(mx_ref.matmul(A[b], X[r]), np.float32(0)) * np.float32(0.05) for b in range(4)]))
            for o in range(4): y[r][:, T * o:T * o + T] += mx_ref.matmul(B[o], H)
    return {"y": y}

from concourse.bass import DstId, RemoteDMATransfer, IndirectOffsetOnAxis
from concourse.mybir import dt, AluOpType, ActivationFunctionType

T_ = 128
HU = 1536
ACT = 512
F8 = "float8_e4m3fn_x4"

SCRATCH = {
    "actb": ("sbuf", [128, 4], "int32"),
    "lst": ("sbuf", [128, 64], "int32"),
    "lf": ("sbuf", [128, 128], "float32"),
    "lt": ("sbuf", [128, 128], "float32"),
    "lc": ("sbuf", [128, 32], "float32"),
    "off": ("sbuf", [128, 128], "uint16"),
    "xb": ("sbuf", [128, 4 * T_], "bfloat16"),
    "w1b": ("sbuf", [128, 4 * HU], "bfloat16"),
    "ab": ("sbuf", [128, 4 * ACT], "bfloat16"),
    "w2g": ("sbuf", [128, 4 * 512], "bfloat16"),
    "bb": ("sbuf", [128, 4 * 512], "bfloat16"),
    "hb": ("sbuf", [128, 4 * 4 * T_], "bfloat16"),
    "xq": ("sbuf", [128, 4 * T_], F8), "xs": ("sbuf", [128, 4 * T_], "uint8"),
    "aq": ("sbuf", [128, ACT], F8), "as_": ("sbuf", [128, ACT], "uint8"),
    "bq": ("sbuf", [128, 512], F8), "bs": ("sbuf", [128, 512], "uint8"),
    "hq": ("sbuf", [128, 4 * T_], F8), "hs": ("sbuf", [128, 4 * T_], "uint8"),
    "hinq": ("sbuf", [128, 4 * T_], F8), "hins": ("sbuf", [128, 4 * T_], "uint8"),
    "binq": ("sbuf", [128, 4 * 512], F8), "bins": ("sbuf", [128, 4 * 512], "uint8"),
    "rlq": ("sbuf", [128, 256], F8), "rls": ("sbuf", [128, 256], "uint8"),
    "ysb": ("sbuf", [128, 4 * T_], "float32"),
    "zp": ("psum", [128, 2048], "float32"),
    "yp": ("psum", [128, 2048], "float32"),
}
SEMAPHORES = (["d_act", "d_x", "d_lst", "d_w1", "ms", "xqd", "lf8", "tr", "lc4", "of4", "ag4", "aqd", "bc4", "bqd", "hr4", "hqd",
               "rc", "rs", "sent", "st0", "st1"]
              + ["sg%d" % t for t in range(4)] + ["z%d" % b for b in range(4)] + ["yo%d" % o for o in range(4)]
              + ["yc%d" % o for o in range(4)]
              + ["x_%d" % s for s in range(4)] + ["h_%d" % s for s in range(4)]
              + ["b0_%d" % s for s in range(4)] + ["b1_%d" % s for s in range(4)])


def bits(es):
    m = 0
    for e in es:
        m |= 1 << e
    return m


def ident(c):
    a = topo_addr[0](c)
    return DstId(rid=a[0], pnc=a[1])


topo_addr = [None]


def relays(me, others, topo):
    far = [c for c in topo.cores_of(me) if topo.die(c) != topo.die(me) and all(topo.may_write(c, d) for d in others)]
    across = [d for d in others if not topo.same_plane(topo.chip(me), topo.chip(d))]
    return [(far[0], across), (far[1], [d for d in others if d not in across])]


def rank_program(g, core, T, topo):
    topo_addr[0] = topo.addr
    rank = T.rank_of(core)
    cores = list(T.cores)
    n = len(cores)
    sem = T.sem
    u8 = dt.uint8

    def copy(src, dsts, to, engines, rsem):
        return RemoteDMATransfer(dst_ids=[ident(c) for c in to], dma_engine_mask=bits(engines), remote_sem=rsem,
                                 srcs=[src], dsts=dsts)

    if rank is None:
        for s in range(n):
            for c, to in relays(cores[s], [d for d in cores if d != cores[s]], topo):
                if c == core:
                    hand_on(g, core, s, to, T, topo, copy)
        return

    others = [(rank + k) % n for k in range(1, n)]
    to = [cores[r] for r in others]
    lo = topo.engines(core, to[0])
    rel = relays(core, to, topo)
    hi = [e for e in topo.engines(core, rel[0][0]) if e not in lo]

    V, S, TE, SY = g.vector, g.scalar, g.tensor, g.sync

    SY.dma_start(T.actb[:], T.act[:]).then_inc(sem.d_act, 16)
    S.dma_start(T.xb[:], T.x[:]).then_inc(sem.d_x, 16)
    SY.dma_start(T.w1b[:], T.w1[:]).then_inc(sem.d_w1, 16)
    V.memset(T.lst[:], 0).then_inc(sem.ms, 1)
    S.wait_ge(sem.ms, 1)
    for q in range(4):
        S.dma_start(T.lst[32 * q:32 * q + 8, :], T.act[:]).then_inc(sem.d_lst, 16)

    g.wait_ge(sem.d_act, 16)
    for t in range(4):
        g.indirect_dma_start(T.w2g[:, 512 * t:512 * t + 512], None, T.w2[:],
                             IndirectOffsetOnAxis(ap=T.actb[:, t:t + 1], axis=0),
                             bounds_check=HU - 1).then_inc(sem["sg%d" % t], 16)
    own = slice(T_ * rank, T_ * rank + T_)
    g.wait_ge(sem.xqd, 1)
    nsent = 0
    g.remote_dma_fused([copy(T.xq[:, own].bitcast(u8), [T.xq[:, own].bitcast(u8)] * 3, to, lo, sem["x_%d" % rank])], local_sem=sem.sent)
    g.remote_dma_fused([copy(T.xs[:, own], [T.xs[:, own]] * 3, to, lo, sem["x_%d" % rank])], local_sem=sem.sent)
    nsent += 2 * len(lo)
    g.wait_ge(sem.bqd, 1)
    base = 512 * rank
    rc = [c for c, _ in rel]
    g.remote_dma_fused([copy(T.bq[:, 256:512].bitcast(u8), [T.rlq[:].bitcast(u8)] * 2, rc, hi, sem.rc),
                        copy(T.bq[:, 0:256].bitcast(u8), [T.binq[:, base:base + 256].bitcast(u8)] * 3, to, lo, sem["b0_%d" % rank])],
                       local_sem=sem.sent)
    g.remote_dma_fused([copy(T.bs[:, 256:512], [T.rls[:]] * 2, rc, hi, sem.rs),
                        copy(T.bs[:, 0:256], [T.bins[:, base:base + 256]] * 3, to, lo, sem["b0_%d" % rank])],
                       local_sem=sem.sent)
    nsent += 2 * (len(lo) + len(hi))
    g.wait_ge(sem.hqd, 1)
    w = 2
    g.remote_dma_fused([copy(T.hq[:, T_ * r:T_ * r + T_].bitcast(u8), [T.hinq[:, own].bitcast(u8)], [cores[r]], lo[w * i:w * i + w],
                             sem["h_%d" % rank]) for i, r in enumerate(others)], local_sem=sem.sent)
    g.remote_dma_fused([copy(T.hs[:, T_ * r:T_ * r + T_], [T.hins[:, own]], [cores[r]], lo[w * i:w * i + w],
                             sem["h_%d" % rank]) for i, r in enumerate(others)], local_sem=sem.sent)
    nsent += 2 * 3 * w
    g.wait_ge(sem.sent, nsent)

    V.wait_ge(sem.d_x, 16)
    V.quantize_mx(T.xq[:, own], T.xs[:, own], T.xb[:]).then_inc(sem.xqd, 1)
    V.wait_ge(sem.d_lst, 64)
    for b in range(4):
        for h in range(2):
            V.tensor_scalar(T.lf[:, 32 * b + 16 * h:32 * b + 16 * h + 16], T.lst[:, b:64:4], 4.0, None, AluOpType.mult).then_inc(sem.lf8, 1)
    V.wait_ge(sem.lf8, 8)
    V.transpose(T.lt[:], T.lf[:]).then_inc(sem.tr, 1)
    V.wait_ge(sem.tr, 1)
    for b in range(4):
        V.tensor_copy(T.lc[:, 8 * b:8 * b + 8], T.lt[:, 32 * b:32 * b + 8]).then_inc(sem.lc4, 1)
    V.wait_ge(sem.lc4, 4)
    for t in range(4):
        V.tensor_scalar(T.off[:, 32 * t:32 * t + 32], T.lc[:], float(t), None, AluOpType.add).then_inc(sem.of4, 1)
    for t in range(4):
        V.wait_ge(sem["sg%d" % t], 16)
        V.tensor_copy(T.bb[:, t:2048:4], T.w2g[:, 512 * t:512 * t + 512]).then_inc(sem.bc4, 1)
    V.wait_ge(sem.bc4, 4)
    V.quantize_mx(T.bq[:], T.bs[:], T.bb[:]).then_inc(sem.bqd, 1)
    V.wait_ge(sem.ag4, 4)
    V.quantize_mx(T.aq[:], T.as_[:], T.ab[:]).then_inc(sem.aqd, 1)
    for b in (1, 3):
        V.wait_ge(sem["z%d" % b], 1)
        V.tensor_scalar(T.hb[:, b:2048:4], T.zp[:, 512 * b:512 * b + 512], 0.05, 0.0, AluOpType.mult, AluOpType.max).then_inc(sem.hr4, 1)
    V.wait_ge(sem.hr4, 4)
    V.quantize_mx(T.hq[:], T.hs[:], T.hb[:]).then_inc(sem.hqd, 1)

    S.wait_ge(sem.of4, 4)
    S.wait_ge(sem.d_w1, 16)
    for t in range(4):
        S.activation(T.ab[:, t:2048:4], T.w1b[:, 0:4 * HU].indirect(T.off[:, 32 * t:32 * t + 32]),
                     ActivationFunctionType.Copy).then_inc(sem.ag4, 1)
    for b in (0, 2):
        S.wait_ge(sem["z%d" % b], 1)
        S.activation(T.hb[:, b:2048:4], T.zp[:, 512 * b:512 * b + 512], ActivationFunctionType.Relu, scale=0.05).then_inc(sem.hr4, 1)

    TE.wait_ge(sem.xqd, 1)
    TE.wait_ge(sem.aqd, 1)
    for r in others:
        TE.wait_ge(sem["x_%d" % r], 2 * len(lo))
    for b in range(4):
        TE.matmul_mx(T.zp[:, 512 * b:512 * b + 512], T.aq[:, 128 * b:128 * b + 128], T.as_[:, 128 * b:128 * b + 128],
                     T.xq[:], T.xs[:], True, True).then_inc(sem["z%d" % b], 1)
    TE.wait_ge(sem.bqd, 1)
    TE.wait_ge(sem.hqd, 1)
    for o in range(4):
        TE.matmul_mx(T.yp[:, 512 * o:512 * o + 128], T.bq[:, 128 * o:128 * o + 128], T.bs[:, 128 * o:128 * o + 128],
                     T.hq[:, own], T.hs[:, own], True, False)
    for s in others:
        TE.wait_ge(sem["h_%d" % s], 2 * w)
    for half in range(2):
        for s in others:
            TE.wait_ge(sem["b%d_%d" % (half, s)], 2 * len(lo))
            for o in (2 * half, 2 * half + 1):
                a = 512 * s + 128 * o
                last = s == others[-1]
                m = TE.matmul_mx(T.yp[:, 512 * o:512 * o + 128], T.binq[:, a:a + 128], T.bins[:, a:a + 128],
                                 T.hinq[:, T_ * s:T_ * s + T_], T.hins[:, T_ * s:T_ * s + T_], False, last)
                if last:
                    m.then_inc(sem["yo%d" % o], 1)

    for half in range(2):
        o = 2 * half
        V.wait_ge(sem["yo%d" % o], 1)
        V.tensor_copy(T.ysb[:, T_ * o:T_ * o + T_], T.yp[:, 512 * o:512 * o + 128]).then_inc(sem["yc%d" % o], 1)
        SY.wait_ge(sem["yc%d" % o], 1)
        SY.dma_start(T.y[:, T_ * o:T_ * o + T_], T.ysb[:, T_ * o:T_ * o + T_]).then_inc(sem.st0, 16)
        o = 2 * half + 1
        S.wait_ge(sem["yo%d" % o], 1)
        S.activation(T.ysb[:, T_ * o:T_ * o + T_], T.yp[:, 512 * o:512 * o + 128], ActivationFunctionType.Copy).then_inc(sem["yc%d" % o], 1)
        S.wait_ge(sem["yc%d" % o], 1)
        S.dma_start(T.y[:, T_ * o:T_ * o + T_], T.ysb[:, T_ * o:T_ * o + T_]).then_inc(sem.st1, 16)
    SY.wait_ge(sem.st0, 32)
    S.wait_ge(sem.st1, 32)


def hand_on(g, core, s, to, T, topo, copy):
    sem = T.sem
    lo = topo.engines(core, to[0])
    me = T.cores[s]
    fed = len([e for e in topo.engines(me, core) if e not in topo.engines(me, to[0])])
    a = 512 * s + 256
    g.wait_ge(sem.rc, fed)
    g.remote_dma_fused([copy(T.rlq[:].bitcast(dt.uint8), [T.binq[:, a:a + 256].bitcast(dt.uint8)] * len(to), to, lo, sem["b1_%d" % s])],
                       local_sem=sem.sent)
    g.wait_ge(sem.rs, fed)
    g.remote_dma_fused([copy(T.rls[:], [T.bins[:, a:a + 256]] * len(to), to, lo, sem["b1_%d" % s])], local_sem=sem.sent)
    g.wait_ge(sem.sent, 2 * len(lo))
